import numpy as np
import ml_dtypes


def mxq(x, axis, fmt="e4m3"):
    dtype, down = {"e4m3": (ml_dtypes.float8_e4m3fn, 7), "e5m2": (ml_dtypes.float8_e5m2, 14)}[fmt]
    v = np.moveaxis(np.asarray(x, np.float32).astype(ml_dtypes.bfloat16).astype(np.float64), axis, -1)
    blocks = v.reshape(v.shape[:-1] + (-1, 32))
    amax = np.abs(blocks).max(-1, keepdims=True)
    byte = np.maximum(np.where(amax > 0, np.frexp(amax)[1] - 1 + 127, 0) - down, 1)
    scale = np.exp2(byte - 127.0)
    codes = (blocks / scale).astype(np.float32).astype(dtype).astype(np.float64)
    return np.moveaxis((codes * scale).reshape(v.shape), -1, axis)


WIDE = False


def mx_kscale(k):
    if not WIDE:
        return np.ones(k)
    levels = np.array([10, -10, 5, -5, 0])
    if k % 512:
        return np.exp2(np.random.permutation(np.resize(levels, k // 32))).repeat(32)
    a = np.empty((k // 512, 16))
    for p in range(k // 512):
        a[p, :8] = np.random.permutation(np.resize(levels, 8))
        for g in range(8):
            far = levels[np.abs(levels - a[p, g]) >= 10]
            a[p, g + 8] = far[np.random.randint(len(far))]
    return np.exp2(a.ravel()).repeat(32)


def f64(x):
    return np.asarray(x).astype(np.float64)


def striped(idx):
    return np.tile(np.asarray(idx).reshape(-1, 16).T, (8, 1)).astype(np.uint16)


def unstriped(offs):
    return offs[:16].T.reshape(-1).astype(np.int64)


E2M1 = np.array([0.0, 0.5, 1.0, 1.5, 2.0, 3.0, 4.0, 6.0, -0.0, -0.5, -1.0, -1.5, -2.0, -3.0, -4.0, -6.0])


def pack_weight(w, fmt):
    k, n = w.shape
    w = f64(np.asarray(w, np.float32).astype(ml_dtypes.bfloat16)).reshape(k // 32, 32, n)
    amax = np.abs(w).max(1)
    if fmt == "e4m3":
        byte = np.frexp(amax)[1] - 1 + 127 - 7
    else:
        mant, ex = np.frexp(amax / 6.0)
        byte = np.where(mant > 0.5, ex, ex - 1) + 127
    byte = np.clip(np.where(amax > 0, byte, 1), 1, 254)
    scaled = (w * np.exp2(127.0 - byte)[:, None, :]).reshape(k, n).astype(np.float32)
    by_word = np.ascontiguousarray(scaled.reshape(k // 512, 128, 4, n).transpose(0, 1, 3, 2))
    if fmt == "e4m3":
        words = by_word.astype(ml_dtypes.float8_e4m3fn).view(np.uint8)
    else:
        c = by_word.astype(ml_dtypes.float4_e2m1fn).view(np.uint8) & 0xF
        words = (c[..., 0::2] | (c[..., 1::2] << 4)).reshape(k // 512, 128, 2 * n)
    return np.ascontiguousarray(words), np.ascontiguousarray(byte.astype(np.uint8).reshape(k // 512, 16, n))


def unpack_weight(words, scales, fmt):
    g, _, n = scales.shape
    words = np.ascontiguousarray(words).reshape(g, 128, n, -1)
    if fmt == "e4m3":
        vals = words.view(ml_dtypes.float8_e4m3fn).astype(np.float64)
    else:
        nib = np.empty((g, 128, n, 4), np.uint8)
        nib[..., 0::2] = words & 0xF
        nib[..., 1::2] = words >> 4
        vals = E2M1[nib]
    vals = vals * np.repeat(np.exp2(scales.astype(np.float64) - 127.0), 8, axis=1)[..., None]
    return vals.transpose(0, 1, 3, 2).reshape(g * 512, n)


D, T, I, Q, E, N, M = 512, 2048, 512, 256, 512, 64, 1024


def setup_inputs():
    n = np.random.standard_normal
    idx = np.random.permutation(T)[:I]
    idx2 = np.random.permutation(M)[:Q]
    fd = mx_kscale(D)
    fi = mx_kscale(I)
    ti = np.ones(T)
    ti[idx] = fi
    keysp = pack_weight(n((D, T)) / fd[:, None], "e2m1")
    return {
        "query": (n((D, Q)) * 0.9 / np.sqrt(D) * fd[:, None]).astype(np.float32),
        "keys_words": keysp[0],
        "keys_scales": keysp[1],
        "lam": (np.random.uniform(0.4, 0.9, (Q, 1))).astype(np.float32),
        "reserve": (np.random.uniform(0.5, 2.0, (Q, 1))).astype(np.float32),
        "os": (np.random.uniform(4.0, 16.0, (1, I)) * fi).astype(np.float32),
        "vals": (n((E, T)) / ti).astype(np.float32),
        "old": (n((E, M)) * 2.0).astype(np.float32),
        "fade": (np.random.uniform(0.3, 0.9, (1, M))).astype(np.float32),
        "offs": striped(idx),
        "offs2": striped(idx2),
    }


def reference(query, keys_words, keys_scales, lam, reserve, os, vals, old, fade, offs, offs2):
    idx = unstriped(offs)
    idx2 = unstriped(offs2)
    keysu = unpack_weight(keys_words, keys_scales, "e2m1")
    queryq = mxq(f64(query), 0, "e4m3")
    keysidxg = keysu[:, idx]
    a = queryq.T @ keysidxg
    mb = a.reshape(Q, N, I // N).max(axis=2)
    mr = np.repeat(mb, I // N, axis=1)
    s = a - mr * f64(lam)
    p = np.exp(s - np.max(s, axis=1, keepdims=True))
    r = p / np.sum(p, axis=1, keepdims=True)
    u0 = r * np.log(r) * (-1.0)
    w = u0 / (np.sum(u0, axis=1, keepdims=True) + f64(reserve))
    wo1 = w * f64(os)
    wt1 = wo1.T
    vt1 = f64(vals)[:, idx].T
    vt1q = mxq(vt1, 0, "e4m3")
    wt1q = mxq(wt1, 0, "e4m3")
    o = vt1q.T @ wt1q
    of = np.zeros((E, M))
    of[:, idx2] = o
    y = f64(old) * f64(fade) + of
    return y

@@ -1,0 +1,293 @@
+from contextlib import ExitStack
+
+import concourse.mybir as mybir
+from concourse.masks import make_identity
+
+D, T, I, Q, E, PAGES, M = 512, 2048, 512, 256, 512, 64, 1024
+FLOPS = 2 * Q * D * I + 2 * E * I * Q
+
+F32 = mybir.dt.float32
+BF16 = mybir.dt.bfloat16
+I32 = mybir.dt.int32
+U32 = mybir.dt.uint32
+U16 = mybir.dt.uint16
+U8 = mybir.dt.uint8
+FP8X4 = mybir.dt.float8_e4m3fn_x4
+FP4X4 = mybir.dt.float4_e2m1fn_x4
+ALU = mybir.AluOpType
+ACT = mybir.ActivationFunctionType
+AXIS = mybir.AxisListType
+
+P = 128
+PACK = 4
+PAGE = I // PAGES
+Q_BLOCKS = Q // P
+E_BLOCKS = E // P
+BANK = 512
+HALVES = M // BANK
+
+
+def tile_attend_pagegap_lacking_written_kernel(
+    tc, query, keys_words, keys_scales, lam, reserve, slot_factor, vals, old, fade, offs, offs2, out
+):
+    nc = tc.nc
+    with ExitStack() as ctx:
+        keep = ctx.enter_context(tc.tile_pool(name="keep", bufs=1))
+        psum = ctx.enter_context(tc.psum_pool(name="psum", bufs=1))
+
+        def bank(tag, name, shape):
+            return psum.tile(shape, F32, name=name, tag=tag)
+
+        def sbuf(name, shape, dtype, tag=None):
+            return keep.tile(shape, dtype, name=name, tag=tag or name, align_bytes=64)
+
+        slot_list = keep.tile([P, I // 16], U16, name="slot_list")
+        column_list = keep.tile([P, Q // 16], U16, name="column_list")
+        key_pool = sbuf("key_pool", [P, T], U16)
+        key_scale_pool = sbuf("key_scale_pool", [P, T], U8)
+        query_rows = sbuf("query_rows", [P, PACK, Q], F32)
+        placed = [sbuf("placed%d" % e, [P, M], F32) for e in range(E_BLOCKS)]
+        lam_less_one = sbuf("lam_less_one", [P, Q_BLOCKS], F32)
+
+        def load_row_values(tile, source):
+            with nc.allow_non_contiguous_dma(reason="one value a query row, rows on the partitions"):
+                nc.sync.dma_start(out=tile[:], in_=source.rearrange("(b p) o -> p (b o)", p=P))
+
+        nc.vector.memset(key_scale_pool[:].bitcast(I32), 0)
+        with tc.tile_pool(name="first", bufs=1) as first:
+            lam_cols = first.tile([P, Q_BLOCKS], F32, name="lam_cols")
+            load_row_values(lam_cols, lam)
+            nc.vector.tensor_scalar(lam_less_one[:], lam_cols[:], -1.0, None, ALU.add)
+        nc.sync.dma_start(out=slot_list[:], in_=offs)
+        nc.sync.dma_start(out=key_pool[:].bitcast(I32), in_=keys_words[0].bitcast(I32))
+        for quad in range(4):
+            nc.sync.dma_start(
+                out=key_scale_pool[32 * quad : 32 * quad + 4, :].bitcast(I32),
+                in_=keys_scales[0, 4 * quad : 4 * quad + 4, :].bitcast(I32),
+            )
+        nc.sync.dma_start(out=query_rows[:], in_=query.rearrange("(p j) q -> p j q", j=PACK))
+        nc.sync.dma_start(out=column_list[:], in_=offs2)
+
+        bulk = ctx.enter_context(tc.tile_pool(name="bulk", bufs=1))
+        value_pool = [bulk.tile([P, T], F32, name="value_pool%d" % e) for e in range(E_BLOCKS)]
+        contents = [bulk.tile([P, M], F32, name="contents%d" % e) for e in range(E_BLOCKS)]
+        reserve_cols = bulk.tile([P, Q_BLOCKS], F32, name="reserve_cols")
+        factor_cols = bulk.tile([P, PACK], F32, name="factor_cols")
+        fade_cols = bulk.tile([P, HALVES, PACK], F32, name="fade_cols")
+
+        def load_values(e):
+            nc.sync.dma_start(out=value_pool[e][:], in_=vals[e * P : (e + 1) * P, :])
+
+        def load_contents(e):
+            nc.sync.dma_start(out=contents[e][:], in_=old[e * P : (e + 1) * P, :])
+
+        load_values(0)
+        load_contents(0)
+        nc.sync.dma_start(out=fade_cols[:], in_=fade.rearrange("o (h n j) -> n (o h) j", h=HALVES, j=PACK))
+        load_row_values(reserve_cols, reserve)
+        nc.sync.dma_start(out=factor_cols[:], in_=slot_factor.rearrange("o (n j) -> n (o j)", j=PACK))
+        load_contents(1)
+        for e in range(1, E_BLOCKS):
+            load_values(e)
+        for e in range(2, E_BLOCKS):
+            load_contents(e)
+
+        for e in range(E_BLOCKS):
+            nc.gpsimd.memset(placed[e][:], 0.0)
+
+        key_codes = sbuf("key_codes", [P, I], U16)
+        key_scales = sbuf("key_scales", [P, I], U8)
+        nc.vector.tensor_copy(out=key_codes[:], in_=key_pool[:].indirect(slot_list[:]))
+        nc.vector.tensor_copy(out=key_scales[:], in_=key_scale_pool[:].indirect(slot_list[:]))
+
+        query_grouped = sbuf("query_grouped", [P, Q, PACK], BF16)
+        nc.scalar.activation(
+            out=query_grouped[:].rearrange("p (c i) j -> p c j i", i=4),
+            in_=query_rows[:].rearrange("p j (c i) -> p c j i", i=4),
+            func=ACT.Copy,
+        )
+        query_codes = sbuf("query_codes", [P, Q], U32)
+        query_scales = sbuf("query_scales", [P, Q], U8)
+        nc.vector.quantize_mx(
+            out=query_codes[:].bitcast(FP8X4),
+            scales=query_scales[:],
+            in_=query_grouped[:].rearrange("p q j -> p (q j)"),
+        )
+
+        identity = sbuf("identity", [P, P], F32, "query_grouped")
+        make_identity(nc, identity[:])
+
+        scores = []
+        for b in range(Q_BLOCKS):
+            cols = slice(b * P, (b + 1) * P)
+            score = bank("AB"[b], "score%d" % b, [P, PAGES, PAGE])
+            nc.tensor.matmul_mx(
+                out=score[:].rearrange("p n i -> p (n i)"),
+                lhsT=query_codes[:, cols].bitcast(FP8X4),
+                lhsT_scale=query_scales[:, cols],
+                rhs=key_codes[:].bitcast(FP4X4),
+                rhs_scale=key_scales[:],
+                start=True,
+                stop=True,
+            )
+            scores.append(score)
+
+        def spread(tag, name, cols):
+            rows = bank(tag, name, [P, PACK, P])
+            for j in range(PACK):
+                nc.tensor.transpose(rows[:, j, :], cols[:, j : j + 1].to_broadcast([P, P]), identity[:])
+            return rows[:].rearrange("p j n -> p n j")
+
+        def turn(source, tag, name, copy):
+            turned = bank(tag, name + "_turned", [P, 2, P])
+            words = source.bitcast(F32)
+            for u in range(2):
+                nc.tensor.transpose(turned[:, u, :], words[:, u : I // 2 : 2], identity[:])
+            grouped = sbuf(name + "_grouped", [P, P * PACK], BF16)
+            copy(
+                out=grouped[:].bitcast(F32).rearrange("p (c u) -> p c u", u=2),
+                in_=turned[:].rearrange("p u c -> p c u"),
+            )
+            return grouped
+
+        value_codes = {}
+        value_scales = {}
+
+        def quantize_values(e, grouped, codes):
+            value_codes[e] = codes
+            value_scales[e] = sbuf("value_scales%d" % e, [P, P], U8)
+            nc.vector.quantize_mx(out=codes.bitcast(FP8X4), scales=value_scales[e][:], in_=grouped[:])
+
+        picked0 = sbuf("picked0", [P, I], BF16)
+        nc.scalar.activation(out=picked0[:], in_=value_pool[0][:].indirect(slot_list[:]), func=ACT.Copy)
+
+        total = sbuf("total", [P, Q_BLOCKS], F32)
+        log_total = sbuf("log_total", [P, Q_BLOCKS], F32)
+        gaps = []
+        shares = []
+        for b in range(Q_BLOCKS):
+            page_max = sbuf("page_max%d" % b, [P, PAGES], F32)
+            page_low = sbuf("page_low%d" % b, [P, PAGES], F32)
+            page_level = sbuf("page_level%d" % b, [P, PAGES], F32)
+            row_low = sbuf("row_low%d" % b, [P, 1], F32)
+            gap = sbuf("gap%d" % b, [P, I], F32)
+            share = sbuf("share%d" % b, [P, I], F32)
+            nc.vector.tensor_reduce(out=page_max[:], in_=scores[b][:], axis=AXIS.X, op=ALU.max)
+            nc.vector.tensor_scalar(
+                page_low[:], page_max[:], lam_less_one[:, b : b + 1], None, ALU.mult, ALU.min, accum_out=row_low[:]
+            )
+            nc.vector.scalar_tensor_tensor(
+                out=page_level[:], in0=page_low[:], scalar=row_low[:], in1=page_max[:], op0=ALU.subtract, op1=ALU.add
+            )
+            nc.vector.tensor_tensor(
+                out=gap[:].rearrange("p (n i) -> p n i", i=PAGE),
+                in0=page_level[:].unsqueeze(2).to_broadcast([P, PAGES, PAGE]),
+                in1=scores[b][:],
+                op=ALU.subtract,
+            )
+            nc.scalar.activation(out=share[:], in_=gap[:], func=ACT.Exp, scale=-1.0, accum_out=total[:, b : b + 1])
+            gaps.append(gap)
+            shares.append(share)
+        nc.scalar.activation(out=log_total[:], in_=total[:], func=ACT.Ln)
+
+        held_back = sbuf("held_back", [P, Q_BLOCKS], F32)
+        nc.gpsimd.tensor_tensor(out=held_back[:], in0=total[:], in1=reserve_cols[:], op=ALU.mult)
+
+        fade_rows = [spread("CD"[h], "fade_rows%d" % h, fade_cols[:, h, :]) for h in range(HALVES)]
+        factor_rows = spread("E", "factor_rows", factor_cols)
+        first_codes = sbuf("first_codes", [P, P], U32, "page_level0")
+        quantize_values(0, turn(picked0[:], "H", "value0", nc.scalar.copy), first_codes[:])
+
+        faded = {}
+
+        def fade_contents(e, h):
+            nc.vector.tensor_tensor(
+                out=faded[e][:, h * BANK : (h + 1) * BANK].rearrange("p (n j) -> p n j", j=PACK),
+                in0=contents[e][:, h * BANK : (h + 1) * BANK].rearrange("p (n j) -> p n j", j=PACK),
+                in1=fade_rows[h],
+                op=ALU.mult,
+            )
+
+        faded_early = sbuf("faded_early", [P, 2 * M], F32, "page_level1")
+        for e in (0, 1):
+            faded[e] = faded_early[:, e * M : (e + 1) * M]
+            for h in range(HALVES):
+                fade_contents(e, h)
+
+        picked_late = sbuf("picked_late", [P, 3 * I], BF16, "total")
+        for e in (1, 2, 3):
+            nc.scalar.activation(
+                out=picked_late[:, (e - 1) * I : e * I], in_=value_pool[e][:].indirect(slot_list[:]), func=ACT.Copy
+            )
+        grouped1 = turn(picked_late[:, 0:I], "H", "value1", nc.scalar.copy)
+
+        weight_codes = sbuf("weight_codes", [P, Q], U32)
+        weight_scales = sbuf("weight_scales", [P, Q], U8)
+        parts = []
+        norms = []
+        for b in range(Q_BLOCKS):
+            part = bulk.tile([P, I], F32, name="part%d" % b, tag="contents%d" % (1 - b))
+            part_sum = sbuf("part_sum%d" % b, [P, 1], F32)
+            divisor = sbuf("divisor%d" % b, [P, 1], F32)
+            norm = sbuf("norm%d" % b, [P, 1], F32)
+            nc.vector.scalar_tensor_tensor(
+                out=part[:], in0=gaps[b][:], scalar=log_total[:, b : b + 1], in1=shares[b][:],
+                op0=ALU.add, op1=ALU.mult, accum_out=part_sum[:],
+            )
+            nc.vector.tensor_tensor(out=divisor[:], in0=part_sum[:], in1=held_back[:, b : b + 1], op=ALU.add)
+            nc.vector.reciprocal(out=norm[:], in_=divisor[:])
+            parts.append(part)
+            norms.append(norm)
+        weights = []
+        for b in range(Q_BLOCKS):
+            weight = sbuf("weight%d" % b, [P, I], BF16)
+            nc.vector.scalar_tensor_tensor(
+                out=weight[:].rearrange("p (n j) -> p n j", j=PACK),
+                in0=parts[b][:].rearrange("p (n j) -> p n j", j=PACK),
+                scalar=norms[b][:],
+                in1=factor_rows,
+                op0=ALU.mult,
+                op1=ALU.mult,
+            )
+            weights.append(weight)
+        for b in range(Q_BLOCKS):
+            cols = slice(b * P, (b + 1) * P)
+            grouped = turn(weights[b][:], "AB"[b], "weight%d" % b, nc.vector.tensor_copy)
+            nc.vector.quantize_mx(
+                out=weight_codes[:, cols].bitcast(FP8X4), scales=weight_scales[:, cols], in_=grouped[:]
+            )
+        late_codes = sbuf("late_codes", [P, 3 * P], U32, "weight0_grouped")
+        quantize_values(1, grouped1, late_codes[:, 0:P])
+        for e in (2, 3):
+            grouped = turn(picked_late[:, (e - 1) * I : e * I], "AB"[e - 2], "value%d" % e, nc.scalar.copy)
+            quantize_values(e, grouped, late_codes[:, (e - 1) * P : e * P])
+
+        read_outs = bulk.tile([P, E_BLOCKS * Q], F32, name="read_outs", tag="value_pool3")
+        for e in range(E_BLOCKS):
+            result = bank("FGEH"[e], "result%d" % e, [P, Q])
+            nc.tensor.matmul_mx(
+                out=result[:],
+                lhsT=value_codes[e].bitcast(FP8X4),
+                lhsT_scale=value_scales[e][:],
+                rhs=weight_codes[:].bitcast(FP8X4),
+                rhs_scale=weight_scales[:],
+                start=True,
+                stop=True,
+            )
+            read_out = read_outs[:, e * Q : (e + 1) * Q]
+            nc.vector.tensor_copy(out=read_out, in_=result[:])
+            nc.scalar.activation(out=placed[e][:].indirect(column_list[:]), in_=read_out, func=ACT.Copy)
+
+        faded_late = sbuf("faded_late", [P, 2 * M], F32, "weight1_grouped")
+        for e in (2, 3):
+            faded[e] = faded_late[:, (e - 2) * M : (e - 1) * M]
+            for h in range(HALVES):
+                fade_contents(e, h)
+
+        for e in range(E_BLOCKS):
+            for h in range(HALVES):
+                cols = slice(h * BANK, (h + 1) * BANK)
+                nc.vector.tensor_tensor(
+                    out=faded[e][:, cols], in0=faded[e][:, cols], in1=placed[e][:, cols], op=ALU.add
+                )
+                nc.sync.dma_start(out=out[e * P : (e + 1) * P, cols], in_=faded[e][:, cols])

@@ -47,17 +47,12 @@ def tile_attend_pagegap_lacking_written_kernel(
         key_scale_pool = sbuf("key_scale_pool", [P, T], U8)
         query_rows = sbuf("query_rows", [P, PACK, Q], F32)
         placed = [sbuf("placed%d" % e, [P, M], F32) for e in range(E_BLOCKS)]
-        lam_less_one = sbuf("lam_less_one", [P, Q_BLOCKS], F32)
 
         def load_row_values(tile, source):
             with nc.allow_non_contiguous_dma(reason="one value a query row, rows on the partitions"):
                 nc.sync.dma_start(out=tile[:], in_=source.rearrange("(b p) o -> p (b o)", p=P))
 
         nc.vector.memset(key_scale_pool[:].bitcast(I32), 0)
-        with tc.tile_pool(name="first", bufs=1) as first:
-            lam_cols = first.tile([P, Q_BLOCKS], F32, name="lam_cols")
-            load_row_values(lam_cols, lam)
-            nc.vector.tensor_scalar(lam_less_one[:], lam_cols[:], -1.0, None, ALU.add)
         nc.sync.dma_start(out=slot_list[:], in_=offs)
         nc.sync.dma_start(out=key_pool[:].bitcast(I32), in_=keys_words[0].bitcast(I32))
         for quad in range(4):
@@ -66,11 +61,12 @@ def tile_attend_pagegap_lacking_written_kernel(
                 in_=keys_scales[0, 4 * quad : 4 * quad + 4, :].bitcast(I32),
             )
         nc.sync.dma_start(out=query_rows[:], in_=query.rearrange("(p j) q -> p j q", j=PACK))
-        nc.sync.dma_start(out=column_list[:], in_=offs2)
+        lam_cols = sbuf("lam_cols", [P, Q_BLOCKS], F32)
+        load_row_values(lam_cols, lam)
 
         bulk = ctx.enter_context(tc.tile_pool(name="bulk", bufs=1))
-        value_pool = [bulk.tile([P, T], F32, name="value_pool%d" % e) for e in range(E_BLOCKS)]
-        contents = [bulk.tile([P, M], F32, name="contents%d" % e) for e in range(E_BLOCKS)]
+        value_pool = [bulk.tile([P, T], F32, name="value_pool%d" % e, align_bytes=64) for e in range(E_BLOCKS)]
+        contents = [bulk.tile([P, M], F32, name="contents%d" % e, align_bytes=64) for e in range(E_BLOCKS)]
         reserve_cols = bulk.tile([P, Q_BLOCKS], F32, name="reserve_cols")
         factor_cols = bulk.tile([P, PACK], F32, name="factor_cols")
         fade_cols = bulk.tile([P, HALVES, PACK], F32, name="fade_cols")
@@ -86,36 +82,39 @@ def tile_attend_pagegap_lacking_written_kernel(
         nc.sync.dma_start(out=fade_cols[:], in_=fade.rearrange("o (h n j) -> n (o h) j", h=HALVES, j=PACK))
         load_row_values(reserve_cols, reserve)
         nc.sync.dma_start(out=factor_cols[:], in_=slot_factor.rearrange("o (n j) -> n (o j)", j=PACK))
+        nc.sync.dma_start(out=column_list[:], in_=offs2)
         load_contents(1)
         for e in range(1, E_BLOCKS):
             load_values(e)
-        for e in range(2, E_BLOCKS):
-            load_contents(e)
+        load_contents(2)
+        load_contents(3)
 
         for e in range(E_BLOCKS):
-            nc.gpsimd.memset(placed[e][:], 0.0)
+            (nc.gpsimd if e < 2 else nc.vector).memset(placed[e][:], 0.0)
 
         key_codes = sbuf("key_codes", [P, I], U16)
         key_scales = sbuf("key_scales", [P, I], U8)
         nc.vector.tensor_copy(out=key_codes[:], in_=key_pool[:].indirect(slot_list[:]))
         nc.vector.tensor_copy(out=key_scales[:], in_=key_scale_pool[:].indirect(slot_list[:]))
 
-        query_grouped = sbuf("query_grouped", [P, Q, PACK], BF16)
-        nc.scalar.activation(
-            out=query_grouped[:].rearrange("p (c i) j -> p c j i", i=4),
-            in_=query_rows[:].rearrange("p j (c i) -> p c j i", i=4),
-            func=ACT.Copy,
-        )
         query_codes = sbuf("query_codes", [P, Q], U32)
         query_scales = sbuf("query_scales", [P, Q], U8)
-        nc.vector.quantize_mx(
-            out=query_codes[:].bitcast(FP8X4),
-            scales=query_scales[:],
-            in_=query_grouped[:].rearrange("p q j -> p (q j)"),
-        )
+        for b in range(Q_BLOCKS):
+            cols = slice(b * P, (b + 1) * P)
+            query_grouped = sbuf("query_grouped%d" % b, [P, P * PACK], BF16)
+            nc.scalar.activation(
+                out=query_grouped[:].rearrange("p (c i j) -> p c j i", i=4, j=PACK),
+                in_=query_rows[:, :, cols].rearrange("p j (c i) -> p c j i", i=4),
+                func=ACT.Copy,
+            )
+            nc.vector.quantize_mx(
+                out=query_codes[:, cols].bitcast(FP8X4), scales=query_scales[:, cols], in_=query_grouped[:]
+            )
 
-        identity = sbuf("identity", [P, P], F32, "query_grouped")
+        identity = sbuf("identity", [P, P], F32, "query_grouped1")
         make_identity(nc, identity[:])
+        lam_less_one = sbuf("lam_less_one", [P, Q_BLOCKS], F32, "query_grouped0")
+        nc.gpsimd.tensor_scalar(lam_less_one[:], lam_cols[:], 1.0, -1.0, ALU.mult, ALU.add)
 
         scores = []
         for b in range(Q_BLOCKS):
@@ -138,17 +137,13 @@ def tile_attend_pagegap_lacking_written_kernel(
                 nc.tensor.transpose(rows[:, j, :], cols[:, j : j + 1].to_broadcast([P, P]), identity[:])
             return rows[:].rearrange("p j n -> p n j")
 
-        def turn(source, tag, name, copy):
+        def turn(source, tag, name, copy, grouped, dealt=False):
             turned = bank(tag, name + "_turned", [P, 2, P])
             words = source.bitcast(F32)
             for u in range(2):
-                nc.tensor.transpose(turned[:, u, :], words[:, u : I // 2 : 2], identity[:])
-            grouped = sbuf(name + "_grouped", [P, P * PACK], BF16)
-            copy(
-                out=grouped[:].bitcast(F32).rearrange("p (c u) -> p c u", u=2),
-                in_=turned[:].rearrange("p u c -> p c u"),
-            )
-            return grouped
+                nc.tensor.transpose(turned[:, u, :], words[:, u * P : (u + 1) * P] if dealt else words[:, u : I // 2 : 2], identity[:])
+            copy(out=grouped.rearrange("p (c u) -> p c u", u=2), in_=turned[:].rearrange("p u c -> p c u"))
+            return grouped.bitcast(BF16)
 
         value_codes = {}
         value_scales = {}
@@ -156,7 +151,7 @@ def tile_attend_pagegap_lacking_written_kernel(
         def quantize_values(e, grouped, codes):
             value_codes[e] = codes
             value_scales[e] = sbuf("value_scales%d" % e, [P, P], U8)
-            nc.vector.quantize_mx(out=codes.bitcast(FP8X4), scales=value_scales[e][:], in_=grouped[:])
+            nc.vector.quantize_mx(out=codes.bitcast(FP8X4), scales=value_scales[e][:], in_=grouped)
 
         picked0 = sbuf("picked0", [P, I], BF16)
         nc.scalar.activation(out=picked0[:], in_=value_pool[0][:].indirect(slot_list[:]), func=ACT.Copy)
@@ -171,7 +166,7 @@ def tile_attend_pagegap_lacking_written_kernel(
             page_level = sbuf("page_level%d" % b, [P, PAGES], F32)
             row_low = sbuf("row_low%d" % b, [P, 1], F32)
             gap = sbuf("gap%d" % b, [P, I], F32)
-            share = sbuf("share%d" % b, [P, I], F32)
+            share = bulk.tile([P, I], F32, name="share%d" % b, tag="value_pool0" if b == 0 else "share1", align_bytes=64)
             nc.vector.tensor_reduce(out=page_max[:], in_=scores[b][:], axis=AXIS.X, op=ALU.max)
             nc.vector.tensor_scalar(
                 page_low[:], page_max[:], lam_less_one[:, b : b + 1], None, ALU.mult, ALU.min, accum_out=row_low[:]
@@ -195,8 +190,7 @@ def tile_attend_pagegap_lacking_written_kernel(
 
         fade_rows = [spread("CD"[h], "fade_rows%d" % h, fade_cols[:, h, :]) for h in range(HALVES)]
         factor_rows = spread("E", "factor_rows", factor_cols)
-        first_codes = sbuf("first_codes", [P, P], U32, "page_level0")
-        quantize_values(0, turn(picked0[:], "H", "value0", nc.scalar.copy), first_codes[:])
+        grouped0 = turn(picked0[:], "F", "value0", nc.scalar.copy, sbuf("value0_grouped", [P, 2 * P], F32)[:])
 
         faded = {}
 
@@ -219,19 +213,19 @@ def tile_attend_pagegap_lacking_written_kernel(
             nc.scalar.activation(
                 out=picked_late[:, (e - 1) * I : e * I], in_=value_pool[e][:].indirect(slot_list[:]), func=ACT.Copy
             )
-        grouped1 = turn(picked_late[:, 0:I], "H", "value1", nc.scalar.copy)
 
         weight_codes = sbuf("weight_codes", [P, Q], U32)
         weight_scales = sbuf("weight_scales", [P, Q], U8)
+        both_parts = bulk.tile([P, Q_BLOCKS * I], F32, name="both_parts", tag="contents1", align_bytes=64)
         parts = []
         norms = []
         for b in range(Q_BLOCKS):
-            part = bulk.tile([P, I], F32, name="part%d" % b, tag="contents%d" % (1 - b))
+            part = both_parts[:, b * I : (b + 1) * I]
             part_sum = sbuf("part_sum%d" % b, [P, 1], F32)
             divisor = sbuf("divisor%d" % b, [P, 1], F32)
             norm = sbuf("norm%d" % b, [P, 1], F32)
             nc.vector.scalar_tensor_tensor(
-                out=part[:], in0=gaps[b][:], scalar=log_total[:, b : b + 1], in1=shares[b][:],
+                out=part, in0=gaps[b][:], scalar=log_total[:, b : b + 1], in1=shares[b][:],
                 op0=ALU.add, op1=ALU.mult, accum_out=part_sum[:],
             )
             nc.vector.tensor_tensor(out=divisor[:], in0=part_sum[:], in1=held_back[:, b : b + 1], op=ALU.add)
@@ -241,53 +235,85 @@ def tile_attend_pagegap_lacking_written_kernel(
         weights = []
         for b in range(Q_BLOCKS):
             weight = sbuf("weight%d" % b, [P, I], BF16)
-            nc.vector.scalar_tensor_tensor(
-                out=weight[:].rearrange("p (n j) -> p n j", j=PACK),
-                in0=parts[b][:].rearrange("p (n j) -> p n j", j=PACK),
-                scalar=norms[b][:],
-                in1=factor_rows,
-                op0=ALU.mult,
-                op1=ALU.mult,
-            )
+            for u in range(2):
+                pair = slice(2 * u, 2 * u + 2)
+                nc.vector.scalar_tensor_tensor(
+                    out=weight[:, u * 2 * P : (u + 1) * 2 * P].rearrange("p (n h) -> p n h", h=2),
+                    in0=parts[b].rearrange("p (n j) -> p n j", j=PACK)[:, :, pair],
+                    scalar=norms[b][:],
+                    in1=factor_rows[:, :, pair],
+                    op0=ALU.mult,
+                    op1=ALU.mult,
+                )
             weights.append(weight)
+        first_codes = bulk.tile([P, P], U32, name="first_codes", tag="contents1", align_bytes=64)
+        quantize_values(0, grouped0, first_codes[:])
         for b in range(Q_BLOCKS):
             cols = slice(b * P, (b + 1) * P)
-            grouped = turn(weights[b][:], "AB"[b], "weight%d" % b, nc.vector.tensor_copy)
+            grouped = turn(weights[b][:], "AB"[b], "weight%d" % b, nc.vector.tensor_copy, sbuf("weight%d_grouped" % b, [P, 2 * P], F32)[:], True)
             nc.vector.quantize_mx(
-                out=weight_codes[:, cols].bitcast(FP8X4), scales=weight_scales[:, cols], in_=grouped[:]
+                out=weight_codes[:, cols].bitcast(FP8X4), scales=weight_scales[:, cols], in_=grouped
             )
-        late_codes = sbuf("late_codes", [P, 3 * P], U32, "weight0_grouped")
-        quantize_values(1, grouped1, late_codes[:, 0:P])
-        for e in (2, 3):
-            grouped = turn(picked_late[:, (e - 1) * I : e * I], "AB"[e - 2], "value%d" % e, nc.scalar.copy)
-            quantize_values(e, grouped, late_codes[:, (e - 1) * P : e * P])
 
-        read_outs = bulk.tile([P, E_BLOCKS * Q], F32, name="read_outs", tag="value_pool3")
-        for e in range(E_BLOCKS):
-            result = bank("FGEH"[e], "result%d" % e, [P, Q])
+        middle = bulk.tile([P, 2 * 2 * P + P], F32, name="middle", tag="value_pool3", align_bytes=64)
+
+        def prepare_values(e):
+            grouped = turn(
+                picked_late[:, (e - 1) * I : e * I],
+                "HGH"[e - 1],
+                "value%d" % e,
+                nc.scalar.copy,
+                sbuf("value3_grouped", [P, 2 * P], F32)[:] if e == 3 else middle[:, (e - 1) * 2 * P : e * 2 * P],
+            )
+            quantize_values(e, grouped, sbuf("value_codes%d" % e, [P, P], U32)[:])
+
+        def place(e, tag, first, count, read_out):
+            result = bank(tag, "result%d_%d" % (e, first), [P, count])
             nc.tensor.matmul_mx(
                 out=result[:],
                 lhsT=value_codes[e].bitcast(FP8X4),
                 lhsT_scale=value_scales[e][:],
-                rhs=weight_codes[:].bitcast(FP8X4),
-                rhs_scale=weight_scales[:],
+                rhs=weight_codes[:, first : first + count].bitcast(FP8X4),
+                rhs_scale=weight_scales[:, first : first + count],
                 start=True,
                 stop=True,
             )
-            read_out = read_outs[:, e * Q : (e + 1) * Q]
             nc.vector.tensor_copy(out=read_out, in_=result[:])
-            nc.scalar.activation(out=placed[e][:].indirect(column_list[:]), in_=read_out, func=ACT.Copy)
+            nc.scalar.activation(
+                out=placed[e][:].indirect(column_list[:, first // 16 : (first + count) // 16]),
+                in_=read_out,
+                func=ACT.Copy,
+            )
 
-        faded_late = sbuf("faded_late", [P, 2 * M], F32, "weight1_grouped")
-        for e in (2, 3):
-            faded[e] = faded_late[:, (e - 2) * M : (e - 1) * M]
-            for h in range(HALVES):
-                fade_contents(e, h)
-
-        for e in range(E_BLOCKS):
-            for h in range(HALVES):
-                cols = slice(h * BANK, (h + 1) * BANK)
+        def finish(e, width):
+            for start in range(0, M, width):
+                cols = slice(start, start + width)
                 nc.vector.tensor_tensor(
                     out=faded[e][:, cols], in0=faded[e][:, cols], in1=placed[e][:, cols], op=ALU.add
                 )
                 nc.sync.dma_start(out=out[e * P : (e + 1) * P, cols], in_=faded[e][:, cols])
+
+        for e in (1, 2, 3):
+            prepare_values(e)
+        def staging(turn_number, count):
+            name = "read_out%d" % turn_number
+            if turn_number % 2 == 0:
+                return bulk.tile([P, count], F32, name=name, tag="value_pool3", align_bytes=64)[:]
+            return sbuf(name, [P, count], F32, "total")[:]
+
+        place(0, "F", 0, P, middle[:, 4 * P :])
+        place(0, "E", P, P, staging(1, P))
+        place(1, "A", 0, Q, staging(2, Q))
+        place(2, "B", 0, Q, staging(3, Q))
+        faded_late = sbuf("faded_late", [P, 2 * M], F32, "weight1_grouped")
+        for e in (2, 3):
+            faded[e] = faded_late[:, (e - 2) * M : (e - 1) * M]
+        for h in range(HALVES):
+            fade_contents(2, h)
+        finish(0, BANK)
+        place(3, "F", 0, Q, staging(4, Q))
+        for h in range(HALVES):
+            fade_contents(3, h)
+        finish(1, BANK)
+        finish(2, BANK)
+        finish(3, BANK // 2)

from contextlib import ExitStack

import concourse.mybir as mybir
from concourse.masks import make_identity

D, T, I, Q, E, PAGES, M = 512, 2048, 512, 256, 512, 64, 1024
FLOPS = 2 * Q * D * I + 2 * E * I * Q

F32 = mybir.dt.float32
BF16 = mybir.dt.bfloat16
I32 = mybir.dt.int32
U32 = mybir.dt.uint32
U16 = mybir.dt.uint16
U8 = mybir.dt.uint8
FP8X4 = mybir.dt.float8_e4m3fn_x4
FP4X4 = mybir.dt.float4_e2m1fn_x4
ALU = mybir.AluOpType
ACT = mybir.ActivationFunctionType
AXIS = mybir.AxisListType

P = 128
PACK = 4
PAGE = I // PAGES
Q_BLOCKS = Q // P
E_BLOCKS = E // P
BANK = 512
HALVES = M // BANK


def tile_attend_pagegap_lacking_written_kernel(
    tc, query, keys_words, keys_scales, lam, reserve, slot_factor, vals, old, fade, offs, offs2, out
):
    nc = tc.nc
    with ExitStack() as ctx:
        keep = ctx.enter_context(tc.tile_pool(name="keep", bufs=1))
        psum = ctx.enter_context(tc.psum_pool(name="psum", bufs=1))

        def bank(tag, name, shape):
            return psum.tile(shape, F32, name=name, tag=tag)

        def sbuf(name, shape, dtype, tag=None):
            return keep.tile(shape, dtype, name=name, tag=tag or name, align_bytes=64)

        slot_list = keep.tile([P, I // 16], U16, name="slot_list")
        column_list = keep.tile([P, Q // 16], U16, name="column_list")
        key_pool = sbuf("key_pool", [P, T], U16)
        key_scale_pool = sbuf("key_scale_pool", [P, T], U8)
        query_rows = sbuf("query_rows", [P, PACK, Q], F32)
        placed = [sbuf("placed%d" % e, [P, M], F32) for e in range(E_BLOCKS)]

        def load_row_values(tile, source):
            with nc.allow_non_contiguous_dma(reason="one value a query row, rows on the partitions"):
                nc.sync.dma_start(out=tile[:], in_=source.rearrange("(b p) o -> p (b o)", p=P))

        nc.vector.memset(key_scale_pool[:].bitcast(I32), 0)
        nc.sync.dma_start(out=slot_list[:], in_=offs)
        nc.sync.dma_start(out=key_pool[:].bitcast(I32), in_=keys_words[0].bitcast(I32))
        for quad in range(4):
            nc.sync.dma_start(
                out=key_scale_pool[32 * quad : 32 * quad + 4, :].bitcast(I32),
                in_=keys_scales[0, 4 * quad : 4 * quad + 4, :].bitcast(I32),
            )
        nc.sync.dma_start(out=query_rows[:], in_=query.rearrange("(p j) q -> p j q", j=PACK))
        lam_cols = sbuf("lam_cols", [P, Q_BLOCKS], F32)
        load_row_values(lam_cols, lam)

        bulk = ctx.enter_context(tc.tile_pool(name="bulk", bufs=1))
        value_pool = [bulk.tile([P, T], F32, name="value_pool%d" % e, align_bytes=64) for e in range(E_BLOCKS)]
        contents = [bulk.tile([P, M], F32, name="contents%d" % e, align_bytes=64) for e in range(E_BLOCKS)]
        reserve_cols = bulk.tile([P, Q_BLOCKS], F32, name="reserve_cols")
        factor_cols = bulk.tile([P, PACK], F32, name="factor_cols")
        fade_cols = bulk.tile([P, HALVES, PACK], F32, name="fade_cols")

        def load_values(e):
            nc.sync.dma_start(out=value_pool[e][:], in_=vals[e * P : (e + 1) * P, :])

        def load_contents(e):
            nc.sync.dma_start(out=contents[e][:], in_=old[e * P : (e + 1) * P, :])

        load_values(0)
        load_contents(0)
        nc.sync.dma_start(out=fade_cols[:], in_=fade.rearrange("o (h n j) -> n (o h) j", h=HALVES, j=PACK))
        load_row_values(reserve_cols, reserve)
        nc.sync.dma_start(out=factor_cols[:], in_=slot_factor.rearrange("o (n j) -> n (o j)", j=PACK))
        nc.sync.dma_start(out=column_list[:], in_=offs2)
        load_contents(1)
        for e in range(1, E_BLOCKS):
            load_values(e)
        load_contents(2)
        load_contents(3)

        for e in range(E_BLOCKS):
            (nc.gpsimd if e < 2 else nc.vector).memset(placed[e][:], 0.0)

        key_codes = sbuf("key_codes", [P, I], U16)
        key_scales = sbuf("key_scales", [P, I], U8)
        nc.vector.tensor_copy(out=key_codes[:], in_=key_pool[:].indirect(slot_list[:]))
        nc.vector.tensor_copy(out=key_scales[:], in_=key_scale_pool[:].indirect(slot_list[:]))

        query_codes = sbuf("query_codes", [P, Q], U32)
        query_scales = sbuf("query_scales", [P, Q], U8)
        for b in range(Q_BLOCKS):
            cols = slice(b * P, (b + 1) * P)
            query_grouped = sbuf("query_grouped%d" % b, [P, P * PACK], BF16)
            nc.scalar.activation(
                out=query_grouped[:].rearrange("p (c i j) -> p c j i", i=4, j=PACK),
                in_=query_rows[:, :, cols].rearrange("p j (c i) -> p c j i", i=4),
                func=ACT.Copy,
            )
            nc.vector.quantize_mx(
                out=query_codes[:, cols].bitcast(FP8X4), scales=query_scales[:, cols], in_=query_grouped[:]
            )

        identity = sbuf("identity", [P, P], F32, "query_grouped1")
        make_identity(nc, identity[:])
        lam_less_one = sbuf("lam_less_one", [P, Q_BLOCKS], F32, "query_grouped0")
        nc.gpsimd.tensor_scalar(lam_less_one[:], lam_cols[:], 1.0, -1.0, ALU.mult, ALU.add)

        scores = []
        for b in range(Q_BLOCKS):
            cols = slice(b * P, (b + 1) * P)
            score = bank("AB"[b], "score%d" % b, [P, PAGES, PAGE])
            nc.tensor.matmul_mx(
                out=score[:].rearrange("p n i -> p (n i)"),
                lhsT=query_codes[:, cols].bitcast(FP8X4),
                lhsT_scale=query_scales[:, cols],
                rhs=key_codes[:].bitcast(FP4X4),
                rhs_scale=key_scales[:],
                start=True,
                stop=True,
            )
            scores.append(score)

        def spread(tag, name, cols):
            rows = bank(tag, name, [P, PACK, P])
            for j in range(PACK):
                nc.tensor.transpose(rows[:, j, :], cols[:, j : j + 1].to_broadcast([P, P]), identity[:])
            return rows[:].rearrange("p j n -> p n j")

        def turn(source, tag, name, copy, grouped, dealt=False):
            turned = bank(tag, name + "_turned", [P, 2, P])
            words = source.bitcast(F32)
            for u in range(2):
                nc.tensor.transpose(turned[:, u, :], words[:, u * P : (u + 1) * P] if dealt else words[:, u : I // 2 : 2], identity[:])
            copy(out=grouped.rearrange("p (c u) -> p c u", u=2), in_=turned[:].rearrange("p u c -> p c u"))
            return grouped.bitcast(BF16)

        value_codes = {}
        value_scales = {}

        def quantize_values(e, grouped, codes):
            value_codes[e] = codes
            value_scales[e] = sbuf("value_scales%d" % e, [P, P], U8)
            nc.vector.quantize_mx(out=codes.bitcast(FP8X4), scales=value_scales[e][:], in_=grouped)

        picked0 = sbuf("picked0", [P, I], BF16)
        nc.scalar.activation(out=picked0[:], in_=value_pool[0][:].indirect(slot_list[:]), func=ACT.Copy)

        total = sbuf("total", [P, Q_BLOCKS], F32)
        log_total = sbuf("log_total", [P, Q_BLOCKS], F32)
        gaps = []
        shares = []
        for b in range(Q_BLOCKS):
            page_max = sbuf("page_max%d" % b, [P, PAGES], F32)
            page_low = sbuf("page_low%d" % b, [P, PAGES], F32)
            page_level = sbuf("page_level%d" % b, [P, PAGES], F32)
            row_low = sbuf("row_low%d" % b, [P, 1], F32)
            gap = sbuf("gap%d" % b, [P, I], F32)
            share = bulk.tile([P, I], F32, name="share%d" % b, tag="value_pool0" if b == 0 else "share1", align_bytes=64)
            nc.vector.tensor_reduce(out=page_max[:], in_=scores[b][:], axis=AXIS.X, op=ALU.max)
            nc.vector.tensor_scalar(
                page_low[:], page_max[:], lam_less_one[:, b : b + 1], None, ALU.mult, ALU.min, accum_out=row_low[:]
            )
            nc.vector.scalar_tensor_tensor(
                out=page_level[:], in0=page_low[:], scalar=row_low[:], in1=page_max[:], op0=ALU.subtract, op1=ALU.add
            )
            nc.vector.tensor_tensor(
                out=gap[:].rearrange("p (n i) -> p n i", i=PAGE),
                in0=page_level[:].unsqueeze(2).to_broadcast([P, PAGES, PAGE]),
                in1=scores[b][:],
                op=ALU.subtract,
            )
            nc.scalar.activation(out=share[:], in_=gap[:], func=ACT.Exp, scale=-1.0, accum_out=total[:, b : b + 1])
            gaps.append(gap)
            shares.append(share)
        nc.scalar.activation(out=log_total[:], in_=total[:], func=ACT.Ln)

        held_back = sbuf("held_back", [P, Q_BLOCKS], F32)
        nc.gpsimd.tensor_tensor(out=held_back[:], in0=total[:], in1=reserve_cols[:], op=ALU.mult)

        fade_rows = [spread("CD"[h], "fade_rows%d" % h, fade_cols[:, h, :]) for h in range(HALVES)]
        factor_rows = spread("E", "factor_rows", factor_cols)
        grouped0 = turn(picked0[:], "F", "value0", nc.scalar.copy, sbuf("value0_grouped", [P, 2 * P], F32)[:])

        faded = {}

        def fade_contents(e, h):
            nc.vector.tensor_tensor(
                out=faded[e][:, h * BANK : (h + 1) * BANK].rearrange("p (n j) -> p n j", j=PACK),
                in0=contents[e][:, h * BANK : (h + 1) * BANK].rearrange("p (n j) -> p n j", j=PACK),
                in1=fade_rows[h],
                op=ALU.mult,
            )

        faded_early = sbuf("faded_early", [P, 2 * M], F32, "page_level1")
        for e in (0, 1):
            faded[e] = faded_early[:, e * M : (e + 1) * M]
            for h in range(HALVES):
                fade_contents(e, h)

        picked_late = sbuf("picked_late", [P, 3 * I], BF16, "total")
        for e in (1, 2, 3):
            nc.scalar.activation(
                out=picked_late[:, (e - 1) * I : e * I], in_=value_pool[e][:].indirect(slot_list[:]), func=ACT.Copy
            )

        weight_codes = sbuf("weight_codes", [P, Q], U32)
        weight_scales = sbuf("weight_scales", [P, Q], U8)
        both_parts = bulk.tile([P, Q_BLOCKS * I], F32, name="both_parts", tag="contents1", align_bytes=64)
        parts = []
        norms = []
        for b in range(Q_BLOCKS):
            part = both_parts[:, b * I : (b + 1) * I]
            part_sum = sbuf("part_sum%d" % b, [P, 1], F32)
            divisor = sbuf("divisor%d" % b, [P, 1], F32)
            norm = sbuf("norm%d" % b, [P, 1], F32)
            nc.vector.scalar_tensor_tensor(
                out=part, in0=gaps[b][:], scalar=log_total[:, b : b + 1], in1=shares[b][:],
                op0=ALU.add, op1=ALU.mult, accum_out=part_sum[:],
            )
            nc.vector.tensor_tensor(out=divisor[:], in0=part_sum[:], in1=held_back[:, b : b + 1], op=ALU.add)
            nc.vector.reciprocal(out=norm[:], in_=divisor[:])
            parts.append(part)
            norms.append(norm)
        weights = []
        for b in range(Q_BLOCKS):
            weight = sbuf("weight%d" % b, [P, I], BF16)
            for u in range(2):
                pair = slice(2 * u, 2 * u + 2)
                nc.vector.scalar_tensor_tensor(
                    out=weight[:, u * 2 * P : (u + 1) * 2 * P].rearrange("p (n h) -> p n h", h=2),
                    in0=parts[b].rearrange("p (n j) -> p n j", j=PACK)[:, :, pair],
                    scalar=norms[b][:],
                    in1=factor_rows[:, :, pair],
                    op0=ALU.mult,
                    op1=ALU.mult,
                )
            weights.append(weight)
        first_codes = bulk.tile([P, P], U32, name="first_codes", tag="contents1", align_bytes=64)
        quantize_values(0, grouped0, first_codes[:])
        for b in range(Q_BLOCKS):
            cols = slice(b * P, (b + 1) * P)
            grouped = turn(weights[b][:], "AB"[b], "weight%d" % b, nc.vector.tensor_copy, sbuf("weight%d_grouped" % b, [P, 2 * P], F32)[:], True)
            nc.vector.quantize_mx(
                out=weight_codes[:, cols].bitcast(FP8X4), scales=weight_scales[:, cols], in_=grouped
            )

        middle = bulk.tile([P, 2 * 2 * P + P], F32, name="middle", tag="value_pool3", align_bytes=64)

        def prepare_values(e):
            grouped = turn(
                picked_late[:, (e - 1) * I : e * I],
                "HGH"[e - 1],
                "value%d" % e,
                nc.scalar.copy,
                sbuf("value3_grouped", [P, 2 * P], F32)[:] if e == 3 else middle[:, (e - 1) * 2 * P : e * 2 * P],
            )
            quantize_values(e, grouped, sbuf("value_codes%d" % e, [P, P], U32)[:])

        def place(e, tag, first, count, read_out):
            result = bank(tag, "result%d_%d" % (e, first), [P, count])
            nc.tensor.matmul_mx(
                out=result[:],
                lhsT=value_codes[e].bitcast(FP8X4),
                lhsT_scale=value_scales[e][:],
                rhs=weight_codes[:, first : first + count].bitcast(FP8X4),
                rhs_scale=weight_scales[:, first : first + count],
                start=True,
                stop=True,
            )
            nc.vector.tensor_copy(out=read_out, in_=result[:])
            nc.scalar.activation(
                out=placed[e][:].indirect(column_list[:, first // 16 : (first + count) // 16]),
                in_=read_out,
                func=ACT.Copy,
            )

        def finish(e, width):
            for start in range(0, M, width):
                cols = slice(start, start + width)
                nc.vector.tensor_tensor(
                    out=faded[e][:, cols], in0=faded[e][:, cols], in1=placed[e][:, cols], op=ALU.add
                )
                nc.sync.dma_start(out=out[e * P : (e + 1) * P, cols], in_=faded[e][:, cols])

        for e in (1, 2, 3):
            prepare_values(e)
        def staging(turn_number, count):
            name = "read_out%d" % turn_number
            if turn_number % 2 == 0:
                return bulk.tile([P, count], F32, name=name, tag="value_pool3", align_bytes=64)[:]
            return sbuf(name, [P, count], F32, "total")[:]

        place(0, "F", 0, P, middle[:, 4 * P :])
        place(0, "E", P, P, staging(1, P))
        place(1, "A", 0, Q, staging(2, Q))
        place(2, "B", 0, Q, staging(3, Q))
        faded_late = sbuf("faded_late", [P, 2 * M], F32, "weight1_grouped")
        for e in (2, 3):
            faded[e] = faded_late[:, (e - 2) * M : (e - 1) * M]
        for h in range(HALVES):
            fade_contents(2, h)
        finish(0, BANK)
        place(3, "F", 0, Q, staging(4, Q))
        for h in range(HALVES):
            fade_contents(3, h)
        finish(1, BANK)
        finish(2, BANK)
        finish(3, BANK // 2)
